import numpy as np
import ml_dtypes

BF16 = ml_dtypes.bfloat16


def bf(x):
    return np.asarray(x, np.float32).astype(BF16)


def f32(x):
    return np.asarray(x, np.float32)


def f64(x):
    return np.asarray(x).astype(np.float64)


def striped(idx):
    return np.tile(idx.reshape(-1, 16).T, (8, 1))


S, K, M, N, D, V = 4096, 128, 256, 1536, 3, 512


def gelu_tanh(v):
    return 0.5 * v * (1.0 + np.tanh(np.sqrt(2.0 / np.pi) * (v + 0.044715 * v**3)))


def setup_inputs():
    return {"table": bf(np.random.standard_normal((S, K))), "w": bf(np.random.standard_normal((D, K, M)) / np.sqrt(D * K)), "b": f32(0.5 * np.random.standard_normal((M, 1))), "offs": striped(np.random.permutation(S)[:N])}


def reference(table, w, b, offs):
    idx = offs[:16].T.reshape(-1)
    x = f64(table)[idx].T
    y = sum(f64(w)[t].T @ x[:, t * V : (t + 1) * V] for t in range(D))
    return gelu_tanh(y + f64(b))

@@ -1,0 +1,87 @@
+import concourse.mybir as mybir
+from concourse.masks import make_identity
+
+P = 128
+S = 4096
+M = 256
+D = 3
+V = 512
+N = D * V
+
+BF16 = mybir.dt.bfloat16
+F32 = mybir.dt.float32
+U16 = mybir.dt.uint16
+
+FLOPS = 2 * P * M * N
+
+LOADS = 4
+BLOCKS_A_LOAD = S // P // LOADS
+BLOCKS_A_GROUP = 4
+GROUP = BLOCKS_A_GROUP * P
+
+
+def tile_gather_matmul_kernel(tc, table, w, b, offs, out):
+    nc = tc.nc
+    with (
+        tc.tile_pool(name="held", bufs=1) as held,
+        tc.tile_pool(name="results", bufs=2) as results,
+        tc.psum_pool(name="flipped", bufs=6) as flipped,
+        tc.psum_pool(name="sums", bufs=2) as sums,
+    ):
+        offsets = held.tile([P, N // 16], U16, name="offsets")
+        nc.sync.dma_start(offsets[:], offs)
+
+        rows = []
+        for load in range(LOADS):
+            rows_tile = held.tile([P, BLOCKS_A_LOAD, P], BF16, name="rows%d" % load)
+            first = load * BLOCKS_A_LOAD * P
+            queue = nc.sync if load % 2 == 0 else nc.scalar
+            queue.dma_start(
+                rows_tile[:],
+                table[first : first + BLOCKS_A_LOAD * P, :].rearrange("(a p) k -> p a k", p=P),
+            )
+            rows.append(rows_tile)
+
+        identity = held.tile([P, P], BF16, name="identity")
+        make_identity(nc, identity[:])
+
+        weights = held.tile([P, D, M], BF16, name="weights")
+        nc.gpsimd.dma_start(weights[:], w.rearrange("t k m -> k t m"))
+        bias = held.tile([P, M // P], F32, name="bias")
+        with nc.allow_non_contiguous_dma(reason="one float32 to a partition for each block of 128 features"):
+            nc.gpsimd.dma_start(bias[:], b.rearrange("(a p) o -> p (a o)", p=P))
+
+        window = held.tile([P, S], BF16, name="window")
+        for group in range(S // GROUP):
+            flip = flipped.tile([P, GROUP], BF16, name="flip")
+            for j in range(BLOCKS_A_GROUP):
+                block = group * BLOCKS_A_GROUP + j
+                nc.tensor.transpose(
+                    flip[:, j * P : (j + 1) * P],
+                    rows[block // BLOCKS_A_LOAD][:, block % BLOCKS_A_LOAD, :],
+                    identity[:],
+                )
+            columns = window[:, group * GROUP : (group + 1) * GROUP]
+            if group % 2 == 0:
+                nc.vector.tensor_copy(columns, flip[:])
+            else:
+                nc.scalar.copy(columns, flip[:])
+
+        for half in range(M // P):
+            total = sums.tile([P, V], F32, name="total")
+            for t in range(D):
+                nc.tensor.matmul(
+                    total[:],
+                    weights[:, t, half * P : (half + 1) * P],
+                    window[:].indirect(offsets[:, t * (V // 16) : (t + 1) * (V // 16)]),
+                    start=(t == 0),
+                    stop=(t == D - 1),
+                )
+            result = results.tile([P, V], F32, name="result")
+            nc.scalar.activation(
+                result[:],
+                total[:],
+                mybir.ActivationFunctionType.Gelu_apprx_tanh,
+                bias=bias[:, half : half + 1],
+            )
+            nc.sync.dma_start(out[half * P : (half + 1) * P, :], result[:])

@@ -14,10 +14,11 @@ U16 = mybir.dt.uint16
 
 FLOPS = 2 * P * M * N
 
+J = 4
+GROUP = J * P
+GROUPS = S // GROUP
 LOADS = 4
-BLOCKS_A_LOAD = S // P // LOADS
-BLOCKS_A_GROUP = 4
-GROUP = BLOCKS_A_GROUP * P
+GROUPS_A_LOAD = GROUPS // LOADS
 
 
 def tile_gather_matmul_kernel(tc, table, w, b, offs, out):
@@ -33,12 +34,12 @@ def tile_gather_matmul_kernel(tc, table, w, b, offs, out):
 
         rows = []
         for load in range(LOADS):
-            rows_tile = held.tile([P, BLOCKS_A_LOAD, P], BF16, name="rows%d" % load)
-            first = load * BLOCKS_A_LOAD * P
+            rows_tile = held.tile([P, GROUPS_A_LOAD, J * P], BF16, name="rows%d" % load)
+            first = load * GROUPS_A_LOAD * GROUP
             queue = nc.sync if load % 2 == 0 else nc.scalar
             queue.dma_start(
                 rows_tile[:],
-                table[first : first + BLOCKS_A_LOAD * P, :].rearrange("(a p) k -> p a k", p=P),
+                table[first : first + GROUPS_A_LOAD * GROUP, :].rearrange("(g p j) k -> p g (j k)", p=P, j=J),
             )
             rows.append(rows_tile)
 
@@ -46,26 +47,30 @@ def tile_gather_matmul_kernel(tc, table, w, b, offs, out):
         make_identity(nc, identity[:])
 
         weights = held.tile([P, D, M], BF16, name="weights")
-        nc.gpsimd.dma_start(weights[:], w.rearrange("t k m -> k t m"))
+        nc.sync.dma_start(weights[:], w.rearrange("t k m -> k t m"))
         bias = held.tile([P, M // P], F32, name="bias")
         with nc.allow_non_contiguous_dma(reason="one float32 to a partition for each block of 128 features"):
-            nc.gpsimd.dma_start(bias[:], b.rearrange("(a p) o -> p (a o)", p=P))
+            nc.scalar.dma_start(bias[:], b.rearrange("(a p) o -> p (a o)", p=P))
+
+        warm = held.tile([P, 1], F32, name="warm")
+        nc.vector.memset(warm[:], 0.0)
+        nc.scalar.activation(warm[:], warm[:], mybir.ActivationFunctionType.Gelu_apprx_tanh)
 
         window = held.tile([P, S], BF16, name="window")
-        for group in range(S // GROUP):
-            flip = flipped.tile([P, GROUP], BF16, name="flip")
-            for j in range(BLOCKS_A_GROUP):
-                block = group * BLOCKS_A_GROUP + j
+        for group in range(GROUPS):
+            flip = flipped.tile([P, J, P], BF16, name="flip")
+            for j in range(J):
                 nc.tensor.transpose(
-                    flip[:, j * P : (j + 1) * P],
-                    rows[block // BLOCKS_A_LOAD][:, block % BLOCKS_A_LOAD, :],
+                    flip[:, j, :],
+                    rows[group // GROUPS_A_LOAD][:, group % GROUPS_A_LOAD, j * P : (j + 1) * P],
                     identity[:],
                 )
-            columns = window[:, group * GROUP : (group + 1) * GROUP]
+            columns = window[:, group * GROUP : (group + 1) * GROUP].rearrange("k (p j) -> k p j", j=J)
+            in_order = flip[:].rearrange("k j p -> k p j")
             if group % 2 == 0:
-                nc.vector.tensor_copy(columns, flip[:])
+                nc.vector.tensor_copy(columns, in_order)
             else:
-                nc.scalar.copy(columns, flip[:])
+                nc.scalar.copy(columns, in_order)
 
         for half in range(M // P):
             total = sums.tile([P, V], F32, name="total")

@@ -19,6 +19,7 @@ GROUP = J * P
 GROUPS = S // GROUP
 LOADS = 4
 GROUPS_A_LOAD = GROUPS // LOADS
+WARM_MATMULS = 4
 
 
 def tile_gather_matmul_kernel(tc, table, w, b, offs, out):
@@ -26,7 +27,8 @@ def tile_gather_matmul_kernel(tc, table, w, b, offs, out):
     with (
         tc.tile_pool(name="held", bufs=1) as held,
         tc.tile_pool(name="results", bufs=2) as results,
-        tc.psum_pool(name="flipped", bufs=6) as flipped,
+        tc.psum_pool(name="flipped", bufs=5) as flipped,
+        tc.psum_pool(name="idle", bufs=1) as idle,
         tc.psum_pool(name="sums", bufs=2) as sums,
     ):
         offsets = held.tile([P, N // 16], U16, name="offsets")
@@ -55,6 +57,12 @@ def tile_gather_matmul_kernel(tc, table, w, b, offs, out):
         warm = held.tile([P, 1], F32, name="warm")
         nc.vector.memset(warm[:], 0.0)
         nc.scalar.activation(warm[:], warm[:], mybir.ActivationFunctionType.Gelu_apprx_tanh)
+
+        zeros = held.tile([P, V], BF16, name="zeros")
+        nc.vector.memset(zeros[:], 0.0)
+        unread = idle.tile([P, V], F32, name="unread")
+        for warm_pass in range(WARM_MATMULS):
+            nc.tensor.matmul(unread[:], zeros[:, 0:P], zeros[:], start=True, stop=True)
 
         window = held.tile([P, S], BF16, name="window")
         for group in range(GROUPS):

@@ -17,7 +17,7 @@ FLOPS = 2 * P * M * N
 J = 4
 GROUP = J * P
 GROUPS = S // GROUP
-LOADS = 4
+LOADS = 8
 GROUPS_A_LOAD = GROUPS // LOADS
 WARM_MATMULS = 4
 
@@ -38,12 +38,17 @@ def tile_gather_matmul_kernel(tc, table, w, b, offs, out):
         for load in range(LOADS):
             rows_tile = held.tile([P, GROUPS_A_LOAD, J * P], BF16, name="rows%d" % load)
             first = load * GROUPS_A_LOAD * GROUP
-            queue = nc.sync if load % 2 == 0 else nc.scalar
-            queue.dma_start(
+            nc.sync.dma_start(
                 rows_tile[:],
                 table[first : first + GROUPS_A_LOAD * GROUP, :].rearrange("(g p j) k -> p g (j k)", p=P, j=J),
             )
             rows.append(rows_tile)
+
+        zeros = held.tile([P, V], BF16, name="zeros")
+        nc.gpsimd.memset(zeros[:], 0.0)
+        unread = idle.tile([P, V], F32, name="unread")
+        for warm_pass in range(WARM_MATMULS):
+            nc.tensor.matmul(unread[:], zeros[:, 0:P], zeros[:], start=True, stop=True)
 
         identity = held.tile([P, P], BF16, name="identity")
         make_identity(nc, identity[:])
@@ -57,12 +62,6 @@ def tile_gather_matmul_kernel(tc, table, w, b, offs, out):
         warm = held.tile([P, 1], F32, name="warm")
         nc.vector.memset(warm[:], 0.0)
         nc.scalar.activation(warm[:], warm[:], mybir.ActivationFunctionType.Gelu_apprx_tanh)
-
-        zeros = held.tile([P, V], BF16, name="zeros")
-        nc.vector.memset(zeros[:], 0.0)
-        unread = idle.tile([P, V], F32, name="unread")
-        for warm_pass in range(WARM_MATMULS):
-            nc.tensor.matmul(unread[:], zeros[:, 0:P], zeros[:], start=True, stop=True)
 
         window = held.tile([P, S], BF16, name="window")
         for group in range(GROUPS):

@@ -19,6 +19,7 @@ GROUP = J * P
 GROUPS = S // GROUP
 LOADS = 8
 GROUPS_A_LOAD = GROUPS // LOADS
+PIECES = 2
 WARM_MATMULS = 4
 
 
@@ -26,7 +27,7 @@ def tile_gather_matmul_kernel(tc, table, w, b, offs, out):
     nc = tc.nc
     with (
         tc.tile_pool(name="held", bufs=1) as held,
-        tc.tile_pool(name="results", bufs=2) as results,
+        tc.tile_pool(name="results", bufs=4) as results,
         tc.psum_pool(name="flipped", bufs=5) as flipped,
         tc.psum_pool(name="idle", bufs=1) as idle,
         tc.psum_pool(name="sums", bufs=2) as sums,
@@ -89,11 +90,13 @@ def tile_gather_matmul_kernel(tc, table, w, b, offs, out):
                     start=(t == 0),
                     stop=(t == D - 1),
                 )
-            result = results.tile([P, V], F32, name="result")
-            nc.scalar.activation(
-                result[:],
-                total[:],
-                mybir.ActivationFunctionType.Gelu_apprx_tanh,
-                bias=bias[:, half : half + 1],
-            )
-            nc.sync.dma_start(out[half * P : (half + 1) * P, :], result[:])
+            for piece in range(PIECES):
+                columns = slice(piece * (V // PIECES), (piece + 1) * (V // PIECES))
+                result = results.tile([P, V // PIECES], F32, name="result")
+                nc.scalar.activation(
+                    result[:],
+                    total[:, columns],
+                    mybir.ActivationFunctionType.Gelu_apprx_tanh,
+                    bias=bias[:, half : half + 1],
+                )
+                nc.sync.dma_start(out[half * P : (half + 1) * P, columns], result[:])

@@ -32,9 +32,6 @@ def tile_gather_matmul_kernel(tc, table, w, b, offs, out):
         tc.psum_pool(name="idle", bufs=1) as idle,
         tc.psum_pool(name="sums", bufs=2) as sums,
     ):
-        offsets = held.tile([P, N // 16], U16, name="offsets")
-        nc.sync.dma_start(offsets[:], offs)
-
         rows = []
         for load in range(LOADS):
             rows_tile = held.tile([P, GROUPS_A_LOAD, J * P], BF16, name="rows%d" % load)
@@ -45,6 +42,14 @@ def tile_gather_matmul_kernel(tc, table, w, b, offs, out):
             )
             rows.append(rows_tile)
 
+        offsets = held.tile([P, N // 16], U16, name="offsets")
+        nc.sync.dma_start(offsets[:], offs)
+        weights = held.tile([P, D, M], BF16, name="weights")
+        nc.sync.dma_start(weights[:], w.rearrange("t k m -> k t m"))
+        bias = held.tile([P, M // P], F32, name="bias")
+        with nc.allow_non_contiguous_dma(reason="one float32 to a partition for each block of 128 features"):
+            nc.sync.dma_start(bias[:], b.rearrange("(a p) o -> p (a o)", p=P))
+
         zeros = held.tile([P, V], BF16, name="zeros")
         nc.gpsimd.memset(zeros[:], 0.0)
         unread = idle.tile([P, V], F32, name="unread")
@@ -53,12 +58,6 @@ def tile_gather_matmul_kernel(tc, table, w, b, offs, out):
 
         identity = held.tile([P, P], BF16, name="identity")
         make_identity(nc, identity[:])
-
-        weights = held.tile([P, D, M], BF16, name="weights")
-        nc.sync.dma_start(weights[:], w.rearrange("t k m -> k t m"))
-        bias = held.tile([P, M // P], F32, name="bias")
-        with nc.allow_non_contiguous_dma(reason="one float32 to a partition for each block of 128 features"):
-            nc.scalar.dma_start(bias[:], b.rearrange("(a p) o -> p (a o)", p=P))
 
         warm = held.tile([P, 1], F32, name="warm")
         nc.vector.memset(warm[:], 0.0)

import concourse.mybir as mybir
from concourse.masks import make_identity

P = 128
S = 4096
M = 256
D = 3
V = 512
N = D * V

BF16 = mybir.dt.bfloat16
F32 = mybir.dt.float32
U16 = mybir.dt.uint16

FLOPS = 2 * P * M * N

J = 4
GROUP = J * P
GROUPS = S // GROUP
LOADS = 8
GROUPS_A_LOAD = GROUPS // LOADS
PIECES = 2
WARM_MATMULS = 4


def tile_gather_matmul_kernel(tc, table, w, b, offs, out):
    nc = tc.nc
    with (
        tc.tile_pool(name="held", bufs=1) as held,
        tc.tile_pool(name="results", bufs=4) as results,
        tc.psum_pool(name="flipped", bufs=5) as flipped,
        tc.psum_pool(name="idle", bufs=1) as idle,
        tc.psum_pool(name="sums", bufs=2) as sums,
    ):
        rows = []
        for load in range(LOADS):
            rows_tile = held.tile([P, GROUPS_A_LOAD, J * P], BF16, name="rows%d" % load)
            first = load * GROUPS_A_LOAD * GROUP
            nc.sync.dma_start(
                rows_tile[:],
                table[first : first + GROUPS_A_LOAD * GROUP, :].rearrange("(g p j) k -> p g (j k)", p=P, j=J),
            )
            rows.append(rows_tile)

        offsets = held.tile([P, N // 16], U16, name="offsets")
        nc.sync.dma_start(offsets[:], offs)
        weights = held.tile([P, D, M], BF16, name="weights")
        nc.sync.dma_start(weights[:], w.rearrange("t k m -> k t m"))
        bias = held.tile([P, M // P], F32, name="bias")
        with nc.allow_non_contiguous_dma(reason="one float32 to a partition for each block of 128 features"):
            nc.sync.dma_start(bias[:], b.rearrange("(a p) o -> p (a o)", p=P))

        zeros = held.tile([P, V], BF16, name="zeros")
        nc.gpsimd.memset(zeros[:], 0.0)
        unread = idle.tile([P, V], F32, name="unread")
        for warm_pass in range(WARM_MATMULS):
            nc.tensor.matmul(unread[:], zeros[:, 0:P], zeros[:], start=True, stop=True)

        identity = held.tile([P, P], BF16, name="identity")
        make_identity(nc, identity[:])

        warm = held.tile([P, 1], F32, name="warm")
        nc.vector.memset(warm[:], 0.0)
        nc.scalar.activation(warm[:], warm[:], mybir.ActivationFunctionType.Gelu_apprx_tanh)

        window = held.tile([P, S], BF16, name="window")
        for group in range(GROUPS):
            flip = flipped.tile([P, J, P], BF16, name="flip")
            for j in range(J):
                nc.tensor.transpose(
                    flip[:, j, :],
                    rows[group // GROUPS_A_LOAD][:, group % GROUPS_A_LOAD, j * P : (j + 1) * P],
                    identity[:],
                )
            columns = window[:, group * GROUP : (group + 1) * GROUP].rearrange("k (p j) -> k p j", j=J)
            in_order = flip[:].rearrange("k j p -> k p j")
            if group % 2 == 0:
                nc.vector.tensor_copy(columns, in_order)
            else:
                nc.scalar.copy(columns, in_order)

        for half in range(M // P):
            total = sums.tile([P, V], F32, name="total")
            for t in range(D):
                nc.tensor.matmul(
                    total[:],
                    weights[:, t, half * P : (half + 1) * P],
                    window[:].indirect(offsets[:, t * (V // 16) : (t + 1) * (V // 16)]),
                    start=(t == 0),
                    stop=(t == D - 1),
                )
            for piece in range(PIECES):
                columns = slice(piece * (V // PIECES), (piece + 1) * (V // PIECES))
                result = results.tile([P, V // PIECES], F32, name="result")
                nc.scalar.activation(
                    result[:],
                    total[:, columns],
                    mybir.ActivationFunctionType.Gelu_apprx_tanh,
                    bias=bias[:, half : half + 1],
                )
                nc.sync.dma_start(out[half * P : (half + 1) * P, columns], result[:])
